import numpy as np
import ml_dtypes


def mxq(x, axis, fmt="e4m3"):
    dtype, down = {"e4m3": (ml_dtypes.float8_e4m3fn, 7), "e5m2": (ml_dtypes.float8_e5m2, 14)}[fmt]
    v = np.moveaxis(np.asarray(x, np.float32).astype(ml_dtypes.bfloat16).astype(np.float64), axis, -1)
    blocks = v.reshape(v.shape[:-1] + (-1, 32))
    amax = np.abs(blocks).max(-1, keepdims=True)
    byte = np.maximum(np.where(amax > 0, np.frexp(amax)[1] - 1 + 127, 0) - down, 1)
    scale = np.exp2(byte - 127.0)
    codes = (blocks / scale).astype(np.float32).astype(dtype).astype(np.float64)
    return np.moveaxis((codes * scale).reshape(v.shape), -1, axis)


WIDE = False


def mx_kscale(k):
    if not WIDE:
        return np.ones(k)
    levels = np.array([10, -10, 5, -5, 0])
    if k % 512:
        return np.exp2(np.random.permutation(np.resize(levels, k // 32))).repeat(32)
    a = np.empty((k // 512, 16))
    for p in range(k // 512):
        a[p, :8] = np.random.permutation(np.resize(levels, 8))
        for g in range(8):
            far = levels[np.abs(levels - a[p, g]) >= 10]
            a[p, g + 8] = far[np.random.randint(len(far))]
    return np.exp2(a.ravel()).repeat(32)


def f64(x):
    return np.asarray(x).astype(np.float64)


def striped8(idx):
    return np.concatenate([x.reshape(-1, 16).T for x in idx]).astype(np.uint16)


def runs(offs, k):
    lists = np.stack([offs[16 * r : 16 * r + 16].T.reshape(-1) for r in range(8)]).astype(np.int64)
    return lists[np.arange(k) % 512 // 64]


def pack_weight(w):
    k, n = w.shape
    w = f64(np.asarray(w, np.float32).astype(ml_dtypes.bfloat16)).reshape(k // 32, 32, n)
    amax = np.abs(w).max(1)
    byte = np.clip(np.where(amax > 0, np.frexp(amax)[1] - 1 + 127 - 7, 1), 1, 254)
    scaled = (w * np.exp2(127.0 - byte)[:, None, :]).reshape(k, n).astype(np.float32)
    words = np.ascontiguousarray(scaled.reshape(k // 512, 128, 4, n).transpose(0, 1, 3, 2)).astype(ml_dtypes.float8_e4m3fn).view(np.uint8)
    return words, np.ascontiguousarray(byte.astype(np.uint8).reshape(k // 512, 16, n))


def unpack_weight(words, scales):
    g, p, n, _ = words.shape
    vals = np.ascontiguousarray(words).view(ml_dtypes.float8_e4m3fn).astype(np.float64) * np.repeat(np.exp2(scales.astype(np.float64) - 127.0), 8, axis=1)[..., None]
    return vals.transpose(0, 1, 3, 2).reshape(g * 512, n)


E2M1 = np.array([0.0, 0.5, 1.0, 1.5, 2.0, 3.0, 4.0, 6.0, -0.0, -0.5, -1.0, -1.5, -2.0, -3.0, -4.0, -6.0])


def pack_fp4(w):
    k, n = w.shape
    w = f64(np.asarray(w, np.float32).astype(ml_dtypes.bfloat16)).reshape(k // 32, 32, n)
    amax = np.abs(w).max(1)
    mant, ex = np.frexp(amax / 6.0)
    byte = np.clip(np.where(amax > 0, np.where(mant > 0.5, ex, ex - 1) + 127, 1), 1, 254)
    scaled = (w * np.exp2(127.0 - byte)[:, None, :]).reshape(k, n).astype(np.float32)
    c = np.ascontiguousarray(scaled.reshape(k // 512, 128, 4, n).transpose(0, 1, 3, 2)).astype(ml_dtypes.float4_e2m1fn).view(np.uint8) & 0xF
    words = (c[..., 0::2] | (c[..., 1::2] << 4)).reshape(k // 512, 128, 2 * n)
    return np.ascontiguousarray(words), np.ascontiguousarray(byte.astype(np.uint8).reshape(k // 512, 16, n))


def unpack_fp4(words, scales):
    g, _, n = scales.shape
    words = np.ascontiguousarray(words).reshape(g, 128, n, 2)
    nib = np.empty((g, 128, n, 4), np.uint8)
    nib[..., 0::2] = words & 0xF
    nib[..., 1::2] = words >> 4
    vals = E2M1[nib] * np.repeat(np.exp2(scales.astype(np.float64) - 127.0), 8, axis=1)[..., None]
    return vals.transpose(0, 1, 3, 2).reshape(g * 512, n)


def sigmoid(v):
    return 1.0 / (1.0 + np.exp(-np.maximum(v, -700.0)))

def planes(y):
    n, m = y.shape
    v = y.astype(np.float32).astype(ml_dtypes.bfloat16).astype(np.float64).reshape(n // 32, 32, m)
    top = np.abs(v).max(1)
    byte = np.clip(np.where(top > 0, np.frexp(top)[1] - 1 + 127 - 7, 1), 1, 254)
    codes = (v * np.exp2(127.0 - byte)[:, None, :]).reshape(n, m).astype(np.float32).astype(ml_dtypes.float8_e4m3fn).view(np.uint8)
    words = codes.reshape(n // 512, 128, 4, m).transpose(0, 1, 3, 2)
    return np.ascontiguousarray(words), np.ascontiguousarray(byte.astype(np.uint8).reshape(n // 512, 16, m))


K, T, S, V, N, G, H = 512, 2048, 512, 256, 512, 2048, 512


def setup_inputs():
    n = np.random.standard_normal
    s = mx_kscale(K)[:, None]
    u = mx_kscale(S)
    packed_xT = pack_weight(n((K, T)) * s)
    packed_dT = pack_weight(n((K, G)) / s)
    packed_w1 = pack_fp4(n((H, N)) / np.sqrt(H) / u[:, None])
    return {
        "x_words": packed_xT[0],
        "x_scales": packed_xT[1],
        "d_words": packed_dT[0],
        "d_scales": packed_dT[1],
        "gn": (np.random.uniform(0.5, 1.5, (H, 1)) * u[:, None]).astype(np.float32),
        "w1_words": packed_w1[0],
        "w1_scales": packed_w1[1],
        "tau": np.random.uniform(0.3, 0.9, (N, 1)).astype(np.float32),
        "tau2": np.random.uniform(0.3, 0.9, (N, 1)).astype(np.float32),
        "offs": striped8(np.random.randint(0, T, (8, S))),
        "k1": striped8(np.random.randint(0, G, (8, H))),
        "n1": striped8(np.stack([np.random.permutation(S) for _ in range(8)])),
        "n2": striped8(np.stack([np.random.permutation(V) for _ in range(8)])),
        "n3": striped8(np.stack([np.random.permutation(V) for _ in range(8)])),
    }


def reference(x_words, x_scales, d_words, d_scales, gn, w1_words, w1_scales, tau, tau2, offs, k1, n1, n2, n3):
    d_k1 = unpack_weight(d_words, d_scales)[np.arange(K)[:, None], runs(k1, K)]
    xq = unpack_weight(x_words, x_scales)[np.arange(K)[:, None], runs(offs, K)]
    h = 0.0625 * (d_k1.T @ xq)
    ln = h[np.arange(H)[:, None], runs(n1, H)]
    mx = ln.reshape(H, V, 2).max(axis=2)
    mn = ln.reshape(H, V, 2).min(axis=2)
    z = f64(gn) * (mx * sigmoid(mn))
    h2 = unpack_fp4(w1_words, w1_scales).T @ mxq(z, 0, "e4m3")
    top = h2.max(axis=1, keepdims=True)
    ea = np.exp(f64(tau) * (h2[np.arange(N)[:, None], runs(n2, N)] - top))
    low = h2.min(axis=1, keepdims=True)
    ea2 = np.exp(f64(tau2) * (low - (h2[np.arange(N)[:, None], runs(n3, N)])))
    out_0 = 1.5 * (h2 * (ea + ea2))
    return (out_0,) + planes(out_0)

@@ -1,0 +1,347 @@
+from contextlib import ExitStack
+
+import concourse.mybir as mybir
+
+FLOPS = 402653184
+
+F32 = mybir.dt.float32
+BF16 = mybir.dt.bfloat16
+I32 = mybir.dt.int32
+U32 = mybir.dt.uint32
+U16 = mybir.dt.uint16
+U8 = mybir.dt.uint8
+FP8X4 = mybir.dt.float8_e4m3fn_x4
+FP4X4 = mybir.dt.float4_e2m1fn_x4
+ALU = mybir.AluOpType
+ACT = mybir.ActivationFunctionType
+AXIS_X = mybir.AxisListType.X
+
+P = 128
+T = 2048
+S = 512
+V = 256
+HALF_S = S // 2
+HALF_V = V // 2
+
+
+def tile_picked_hpqhpgateedf_none_po_kernel(
+    tc, x_words, x_scales, d_words, d_scales, gn, w1_words, w1_scales, tau, tau2,
+    offs, k1, n1, n2, n3, out_0, out_1, out_2,
+):
+    nc = tc.nc
+    with ExitStack() as ctx:
+        lists = ctx.enter_context(tc.tile_pool(name="lists", bufs=1))
+        sb = ctx.enter_context(tc.tile_pool(name="sb", bufs=1))
+        ps = ctx.enter_context(tc.psum_pool(name="ps", bufs=1))
+
+        def tile(name, shape, dtype, tag=None):
+            return sb.tile(shape, dtype, name=name, tag=tag or name, align_bytes=64)
+
+        def bank(b, name, shape):
+            return ps.tile(shape, F32, name=name, tag="bank%d" % b)
+
+        d_sc_win = tile("d_sc_win", [P, T], U8)
+        x_sc_win = tile("x_sc_win", [P, T], U8)
+        nc.vector.memset(d_sc_win[:].bitcast(I32), 0)
+        nc.scalar.dma_start(d_sc_win[0:P:8, :].bitcast(I32), d_scales[0].bitcast(I32))
+        nc.vector.memset(x_sc_win[:].bitcast(I32), 0)
+        nc.scalar.dma_start(x_sc_win[0:P:8, :].bitcast(I32), x_scales[0].bitcast(I32))
+
+        k1_l = lists.tile([P, S // 16], U16, name="k1_l")
+        offs_l = lists.tile([P, S // 16], U16, name="offs_l")
+        n1_l = lists.tile([P, S // 16], U16, name="n1_l")
+        n2_l = lists.tile([P, V // 16], U16, name="n2_l")
+        n3_l = lists.tile([P, V // 16], U16, name="n3_l")
+        for lst, src in ((k1_l, k1), (offs_l, offs), (n1_l, n1), (n2_l, n2), (n3_l, n3)):
+            nc.sync.dma_start(lst[:], src)
+        d_win = tile("d_win", [P, T], U32)
+        x_win = tile("x_win", [P, T], U32)
+        nc.sync.dma_start(d_win[:].bitcast(I32), d_words[0].rearrange("p n r -> p (n r)").bitcast(I32))
+        nc.sync.dma_start(x_win[:].bitcast(I32), x_words[0].rearrange("p n r -> p (n r)").bitcast(I32))
+
+        tau_sb = tile("tau_sb", [P, 4], F32)
+        tau2_sb = tile("tau2_sb", [P, 4], F32)
+        gn_sb = tile("gn_sb", [P, 4], F32)
+        w_raw = tile("w_raw", [P, 2 * S], U8)
+        nc.gpsimd.dma_start(tau_sb[:], tau.rearrange("(p t) o -> p (t o)", t=4))
+        nc.gpsimd.dma_start(tau2_sb[:], tau2.rearrange("(p t) o -> p (t o)", t=4))
+        nc.gpsimd.dma_start(w_raw[:].bitcast(I32), w1_words[0].bitcast(I32))
+        nc.gpsimd.dma_start(gn_sb[:], gn.rearrange("(p t) o -> p (t o)", t=4))
+
+        scales = tile("scales", [P, 2 * S], U8)
+        nc.vector.memset(scales[:].bitcast(I32), 0)
+        h2_win = [tile("h2_win%d" % t, [P, 2 * V], F32) for t in range(4)]
+        for t in range(4):
+            nc.vector.memset(h2_win[t][:, V:], 0.0)
+
+        neg_tau = tile("neg_tau", [P, 4], F32)
+        neg_tau2 = tile("neg_tau2", [P, 4], F32)
+        nc.scalar.activation(neg_tau[:], tau_sb[:], ACT.Copy, scale=-1.0)
+        nc.scalar.activation(neg_tau2[:], tau2_sb[:], ACT.Copy, scale=-1.0)
+
+        d_sc_got = tile("d_sc_got", [P, S], U8)
+        x_sc_got = tile("x_sc_got", [P, S], U8)
+        staged = tile("staged", [P, 2 * S], U8)
+        nc.vector.tensor_copy(d_sc_got[:], d_sc_win[:].indirect(k1_l[:]))
+        nc.vector.tensor_copy(x_sc_got[:], x_sc_win[:].indirect(offs_l[:]))
+        nc.vector.tensor_copy(
+            staged[:, S:].rearrange("p (t c i) -> p c t i", t=4, i=16),
+            d_sc_got[:].rearrange("p (c i t) -> p c t i", t=4, i=16),
+        )
+        nc.vector.tensor_copy(staged[:, :S].bitcast(I32), x_sc_got[:].bitcast(I32))
+        for r in range(4):
+            nc.scalar.dma_start(scales[r:P:32, :].bitcast(I32), staged[8 * r : P : 32, :].bitcast(I32))
+
+        w_sc_raw = tile("w_sc_raw", [P, S], U8, tag="staged")
+        nc.gpsimd.memset(w_sc_raw[:].bitcast(I32), 0)
+        for q in range(4):
+            nc.sync.dma_start(
+                w_sc_raw[32 * q : 32 * q + 4, :].bitcast(I32), w1_scales[0, 4 * q : 4 * q + 4, :].bitcast(I32)
+            )
+
+        d_got = tile("d_got", [P, S], U32)
+        d_dealt = tile("d_dealt", [P, S], U32)
+        nc.vector.tensor_copy(d_got[:], d_win[:].indirect(k1_l[:]))
+        x_got = [tile("x_got%d" % a, [P, HALF_S], U32) for a in range(2)]
+        nc.vector.tensor_copy(x_got[0][:], x_win[:].indirect(offs_l[:, :16]))
+        nc.vector.tensor_copy(
+            d_dealt[:].bitcast(I32).rearrange("p (t c i) -> p c t i", t=4, i=4),
+            d_got[:].bitcast(I32).rearrange("p (c i t) -> p c t i", t=4, i=4),
+        )
+        nc.vector.tensor_copy(x_got[1][:], x_win[:].indirect(offs_l[:, 16:]))
+
+        w_dealt = tile("w_dealt", [P, 2 * S], U8)
+        nc.scalar.copy(
+            w_dealt[:].bitcast(U16).rearrange("p (t c i) -> p c t i", t=4, i=8),
+            w_raw[:].bitcast(U16).rearrange("p (c i t) -> p c t i", t=4, i=8),
+        )
+
+        h_win = [tile("h_win%d" % t, [P, S], F32) for t in range(4)]
+        for a, t in ((0, 0), (0, 1), (1, 0), (1, 1), (0, 2), (1, 2), (0, 3), (1, 3)):
+            cols = slice(a * HALF_S, (a + 1) * HALF_S)
+            acc = bank(4 * a + t, "h_acc", [P, HALF_S])
+            nc.tensor.matmul_mx(
+                acc[:],
+                lhsT=d_dealt[:, P * t : P * (t + 1)].bitcast(FP8X4),
+                lhsT_scale=scales[:, S + P * t : S + P * (t + 1)],
+                rhs=x_got[a][:].bitcast(FP8X4),
+                rhs_scale=scales[:, cols],
+                start=True,
+                stop=True,
+            )
+            if a == 0 and t < 2:
+                nc.scalar.activation(h_win[t][:, cols], acc[:], ACT.Copy, scale=0.03125)
+            else:
+                nc.vector.tensor_scalar(h_win[t][:, cols], acc[:], 0.03125, None, ALU.mult)
+
+        lined = tile("lined", [P, 4, HALF_S], F32)
+        small_first = tile("small_first", [P, 4, HALF_V], F32)
+        large = tile("large", [P, 4, HALF_V], F32)
+        tanh = [tile("tanh%d" % a, [P, 4, HALF_V], F32) for a in range(2)]
+        gate = tile("gate", [P, 4, HALF_V], F32)
+
+        def small(a, ts):
+            if a == 0:
+                return small_first[:, ts, :]
+            if ts.start < 3:
+                return tanh[0][:, ts.start + 1 : ts.stop + 1, :]
+            return gate[:, ts, :]
+        z_bf = [tile("z_bf%d" % a, [P, HALF_V, 4], BF16) for a in range(2)]
+        z_codes = [tile("z_codes%d" % a, [P, HALF_V], U32) for a in range(2)]
+        z_scales = [tile("z_scales%d" % a, [P, HALF_V], U8) for a in range(2)]
+
+        def line_up(a, t):
+            nc.scalar.activation(lined[:, t, :], h_win[t][:].indirect(n1_l[:, 16 * a : 16 * (a + 1)]), ACT.Copy)
+
+        def pick_small(a, ts):
+            nc.vector.tensor_tensor(small(a, ts), lined[:, ts, 0::2], lined[:, ts, 1::2], ALU.min)
+
+        def pick_large(ts):
+            nc.vector.tensor_tensor(large[:, ts, :], lined[:, ts, 0::2], lined[:, ts, 1::2], ALU.max)
+
+        def squash(a, ts):
+            nc.scalar.activation(tanh[a][:, ts, :], small(a, ts), ACT.Tanh)
+
+        def gain(a, t):
+            nc.vector.tensor_scalar(gate[:, t, :], tanh[a][:, t, :], 1.0, gn_sb[:, t : t + 1], ALU.add, ALU.mult)
+
+        def make_z(a):
+            nc.vector.tensor_tensor(
+                z_bf[a][:].rearrange("p (c i) t -> p c t i", i=4),
+                gate[:].rearrange("p t (c i) -> p c t i", i=4),
+                large[:].rearrange("p t (c i) -> p c t i", i=4),
+                ALU.mult,
+            )
+
+        def quantise_z(a):
+            nc.vector.quantize_mx(
+                z_codes[a][:].bitcast(FP8X4), z_scales[a][:], z_bf[a][:].rearrange("p v t -> p (v t)")
+            )
+
+        def second(acc, a, t):
+            nc.tensor.matmul_mx(
+                acc,
+                lhsT=w_dealt[:, 2 * P * t : 2 * P * (t + 1)].bitcast(FP4X4),
+                lhsT_scale=w_sc[:, P * t : P * (t + 1)],
+                rhs=z_codes[a][:].bitcast(FP8X4),
+                rhs_scale=z_scales[a][:],
+                start=True,
+                stop=True,
+            )
+
+        every, front, back = slice(0, 4), slice(0, 2), slice(2, 4)
+        for t in range(4):
+            line_up(0, t)
+        pick_small(0, front)
+        pick_large(front)
+        w_sc = tile("w_sc", [P, S], U8, tag="d_dealt")
+        nc.vector.tensor_copy(
+            w_sc[:].rearrange("p (t c i) -> p c t i", t=4, i=16),
+            w_sc_raw[:].rearrange("p (c i t) -> p c t i", t=4, i=16),
+        )
+        pick_small(0, back)
+        pick_large(back)
+        squash(0, front)
+        line_up(1, 0)
+        squash(0, back)
+        for t in range(1, 4):
+            line_up(1, t)
+        for t in range(4):
+            gain(0, t)
+        pick_small(1, slice(0, 1))
+        make_z(0)
+        pick_small(1, slice(1, 3))
+        quantise_z(0)
+        h2_a = bank(0, "h2_a", [P, 4, HALF_V])
+        for t in range(4):
+            second(h2_a[:, t, :], 0, t)
+        pick_small(1, slice(3, 4))
+        pick_large(every)
+        squash(1, slice(0, 3))
+        squash(1, slice(3, 4))
+        for t in range(4):
+            gain(1, t)
+
+        top_a = tile("top_a", [P, 4], F32)
+        top = tile("top", [P, 4], F32)
+        low_a = tile("low_a", [P, 4], F32)
+        low_b = tile("low_b", [P, 4], F32)
+        low = tile("low", [P, 4], F32)
+        bias_top = tile("bias_top", [P, 4], F32)
+        bias_low = tile("bias_low", [P, 4], F32)
+        ea = tile("ea", [P, 4, V], F32)
+        eb = tile("eb", [P, 4, V], F32)
+        both = tile("both", [P, 4, V], F32)
+        res = tile("res", [P, 4, V], F32)
+        res_bf = tile("res_bf", [P, V, 4], BF16)
+        out_codes = tile("out_codes", [P, V], U32)
+        out_scales = tile("out_scales", [P, V], U8)
+        out_rows = out_0.rearrange("(p t) v -> p t v", t=4)
+        out_words = out_1[0].rearrange("p v r -> p (v r)").bitcast(I32)
+        first, last, whole = slice(0, HALF_V), slice(HALF_V, V), slice(0, V)
+
+        def keep_first(t):
+            nc.vector.tensor_scalar(
+                h2_win[t][:, first], h2_a[:, t, :], 1.0, None, ALU.mult, ALU.max, accum_out=top_a[:, t : t + 1]
+            )
+
+        def keep_last(t):
+            nc.vector.tensor_scalar(
+                h2_win[t][:, last], h2_b[t // 2][:, t % 2, :], 1.0, top_a[:, t : t + 1], ALU.mult, ALU.max,
+                accum_out=top[:, t : t + 1],
+            )
+
+        def top_bias(ts):
+            nc.vector.tensor_tensor(bias_top[:, ts], top[:, ts], neg_tau[:, ts], ALU.mult)
+
+        def lowest_last(ts):
+            nc.vector.tensor_reduce(low_b[:, ts], h2_b[ts.start // 2][:], AXIS_X, ALU.min)
+
+        def lowest(ts):
+            nc.vector.tensor_tensor(low[:, ts], low_a[:, ts], low_b[:, ts], ALU.min)
+
+        def low_bias(ts):
+            nc.vector.tensor_tensor(bias_low[:, ts], low[:, ts], tau2_sb[:, ts], ALU.mult)
+
+        def fetch_top(t):
+            nc.scalar.activation(
+                ea[:, t, :], h2_win[t][:].indirect(n2_l[:]), ACT.Exp,
+                bias=bias_top[:, t : t + 1], scale=tau_sb[:, t : t + 1],
+            )
+
+        def fetch_low(t, cols):
+            nc.scalar.activation(
+                eb[:, t, cols], h2_win[t][:].indirect(n3_l[:, cols.start // 16 : cols.stop // 16]), ACT.Exp,
+                bias=bias_low[:, t : t + 1], scale=neg_tau2[:, t : t + 1],
+            )
+
+        def add_both(ts, cols):
+            nc.vector.tensor_tensor(both[:, ts, cols], ea[:, ts, cols], eb[:, ts, cols], ALU.add)
+
+        def finish(ts, cols, h2):
+            nc.vector.scalar_tensor_tensor(res[:, ts, cols], h2, 1.5, both[:, ts, cols], ALU.mult, ALU.mult)
+
+        def round_res(copy, ts, cols):
+            copy(
+                res_bf[:, cols, ts].rearrange("p (c i) t -> p c t i", i=4),
+                res[:, ts, cols].rearrange("p t (c i) -> p c t i", i=4),
+            )
+
+        def planes(cols):
+            nc.vector.quantize_mx(
+                out_codes[:, cols].bitcast(FP8X4), out_scales[:, cols],
+                res_bf[:, cols, :].rearrange("p v t -> p (v t)"),
+            )
+            nc.sync.dma_start(out_words[:, cols], out_codes[:, cols].bitcast(I32))
+
+        keep_first(0)
+        make_z(1)
+        keep_first(1)
+        quantise_z(1)
+        h2_b = [bank(1 + u, "h2_b", [P, 2, HALF_V]) for u in range(2)]
+        for t in range(4):
+            second(h2_b[t // 2][:, t % 2, :], 1, t)
+        nc.vector.tensor_reduce(low_a[:], h2_a[:], AXIS_X, ALU.min)
+        keep_last(0)
+        keep_last(1)
+        top_bias(slice(0, 1))
+        top_bias(slice(1, 2))
+        fetch_top(0)
+        fetch_top(1)
+        lowest_last(front)
+        keep_first(2)
+        lowest(front)
+        keep_first(3)
+        low_bias(front)
+        fetch_low(0, whole)
+        fetch_low(1, whole)
+        keep_last(2)
+        keep_last(3)
+        lowest_last(back)
+        top_bias(back)
+        lowest(back)
+        fetch_top(2)
+        fetch_top(3)
+        add_both(front, whole)
+        low_bias(back)
+        for cols in (first, last):
+            fetch_low(2, cols)
+            fetch_low(3, cols)
+        finish(front, first, h2_a[:, front, :])
+        finish(front, last, h2_b[0][:])
+        nc.sync.dma_start(out_rows[:, front, :], res[:, front, :])
+        round_res(nc.vector.tensor_copy, front, whole)
+        add_both(back, first)
+        add_both(slice(2, 3), last)
+        finish(back, first, h2_a[:, back, :])
+        nc.sync.dma_start(out_rows[:, back, first], res[:, back, first])
+        add_both(slice(3, 4), last)
+        round_res(nc.scalar.copy, back, first)
+        finish(back, last, h2_b[1][:])
+        nc.sync.dma_start(out_rows[:, back, last], res[:, back, last])
+        planes(first)
+        round_res(nc.scalar.copy, back, last)
+        planes(last)
+        for q in range(4):
+            eng = nc.scalar if q % 2 == 0 else nc.sync
+            eng.dma_start(out_2[0, 4 * q : 4 * q + 4, :].bitcast(I32), out_scales[32 * q : 32 * q + 4, :].bitcast(I32))

@@ -40,59 +40,51 @@ def tile_picked_hpqhpgateedf_none_po_kernel(
         def bank(b, name, shape):
             return ps.tile(shape, F32, name=name, tag="bank%d" % b)
 
-        d_sc_win = tile("d_sc_win", [P, T], U8)
-        x_sc_win = tile("x_sc_win", [P, T], U8)
-        nc.vector.memset(d_sc_win[:].bitcast(I32), 0)
-        nc.scalar.dma_start(d_sc_win[0:P:8, :].bitcast(I32), d_scales[0].bitcast(I32))
-        nc.vector.memset(x_sc_win[:].bitcast(I32), 0)
-        nc.scalar.dma_start(x_sc_win[0:P:8, :].bitcast(I32), x_scales[0].bitcast(I32))
-
         k1_l = lists.tile([P, S // 16], U16, name="k1_l")
         offs_l = lists.tile([P, S // 16], U16, name="offs_l")
         n1_l = lists.tile([P, S // 16], U16, name="n1_l")
         n2_l = lists.tile([P, V // 16], U16, name="n2_l")
         n3_l = lists.tile([P, V // 16], U16, name="n3_l")
-        for lst, src in ((k1_l, k1), (offs_l, offs), (n1_l, n1), (n2_l, n2), (n3_l, n3)):
-            nc.sync.dma_start(lst[:], src)
-        d_win = tile("d_win", [P, T], U32)
-        x_win = tile("x_win", [P, T], U32)
-        nc.sync.dma_start(d_win[:].bitcast(I32), d_words[0].rearrange("p n r -> p (n r)").bitcast(I32))
-        nc.sync.dma_start(x_win[:].bitcast(I32), x_words[0].rearrange("p n r -> p (n r)").bitcast(I32))
-
+        d_sc_win = tile("d_sc_win", [P, T], U8)
+        x_sc_win = tile("x_sc_win", [P, T], U8)
+        nc.gpsimd.memset(d_sc_win[:].bitcast(I32), 0)
+        nc.scalar.dma_start(d_sc_win[0:P:8, :].bitcast(I32), d_scales[0].bitcast(I32))
+        nc.vector.memset(x_sc_win[:].bitcast(I32), 0)
+        nc.scalar.dma_start(x_sc_win[0:P:8, :].bitcast(I32), x_scales[0].bitcast(I32))
         tau_sb = tile("tau_sb", [P, 4], F32)
         tau2_sb = tile("tau2_sb", [P, 4], F32)
         gn_sb = tile("gn_sb", [P, 4], F32)
+        for lst, src in ((k1_l, k1), (offs_l, offs), (n1_l, n1), (n2_l, n2), (n3_l, n3)):
+            nc.sync.dma_start(lst[:], src)
+        nc.sync.dma_start(tau_sb[:], tau.rearrange("(p t) o -> p (t o)", t=4))
+
+        d_win = tile("d_win", [P, T], U32)
+        x_win = tile("x_win", [P, T], U32)
         w_raw = tile("w_raw", [P, 2 * S], U8)
-        nc.gpsimd.dma_start(tau_sb[:], tau.rearrange("(p t) o -> p (t o)", t=4))
-        nc.gpsimd.dma_start(tau2_sb[:], tau2.rearrange("(p t) o -> p (t o)", t=4))
+        nc.gpsimd.dma_start(d_win[:].bitcast(I32), d_words[0].rearrange("p n r -> p (n r)").bitcast(I32))
+        nc.gpsimd.dma_start(x_win[:].bitcast(I32), x_words[0].rearrange("p n r -> p (n r)").bitcast(I32))
         nc.gpsimd.dma_start(w_raw[:].bitcast(I32), w1_words[0].bitcast(I32))
         nc.gpsimd.dma_start(gn_sb[:], gn.rearrange("(p t) o -> p (t o)", t=4))
+        nc.gpsimd.dma_start(tau2_sb[:], tau2.rearrange("(p t) o -> p (t o)", t=4))
 
-        scales = tile("scales", [P, 2 * S], U8)
-        nc.vector.memset(scales[:].bitcast(I32), 0)
-        h2_win = [tile("h2_win%d" % t, [P, 2 * V], F32) for t in range(4)]
-        for t in range(4):
-            nc.vector.memset(h2_win[t][:, V:], 0.0)
+        d_sc_placed = tile("d_sc_placed", [P, S], U8)
+        x_sc = tile("x_sc", [P, S], U8)
+        nc.vector.memset(d_sc_placed[:].bitcast(I32), 0)
+        nc.vector.memset(x_sc[:].bitcast(I32), 0)
 
         neg_tau = tile("neg_tau", [P, 4], F32)
         neg_tau2 = tile("neg_tau2", [P, 4], F32)
         nc.scalar.activation(neg_tau[:], tau_sb[:], ACT.Copy, scale=-1.0)
-        nc.scalar.activation(neg_tau2[:], tau2_sb[:], ACT.Copy, scale=-1.0)
+        nc.gpsimd.tensor_scalar(neg_tau2[:], tau2_sb[:], -1.0, 0.0, ALU.mult, ALU.add)
 
         d_sc_got = tile("d_sc_got", [P, S], U8)
         x_sc_got = tile("x_sc_got", [P, S], U8)
-        staged = tile("staged", [P, 2 * S], U8)
-        nc.vector.tensor_copy(d_sc_got[:], d_sc_win[:].indirect(k1_l[:]))
-        nc.vector.tensor_copy(x_sc_got[:], x_sc_win[:].indirect(offs_l[:]))
-        nc.vector.tensor_copy(
-            staged[:, S:].rearrange("p (t c i) -> p c t i", t=4, i=16),
-            d_sc_got[:].rearrange("p (c i t) -> p c t i", t=4, i=16),
-        )
-        nc.vector.tensor_copy(staged[:, :S].bitcast(I32), x_sc_got[:].bitcast(I32))
-        for r in range(4):
-            nc.scalar.dma_start(scales[r:P:32, :].bitcast(I32), staged[8 * r : P : 32, :].bitcast(I32))
+        for got, win, lst, placed in ((d_sc_got, d_sc_win, k1_l, d_sc_placed), (x_sc_got, x_sc_win, offs_l, x_sc)):
+            nc.vector.tensor_copy(got[:], win[:].indirect(lst[:]))
+            for r in range(4):
+                nc.sync.dma_start(placed[r:P:32, :].bitcast(I32), got[8 * r : P : 32, :].bitcast(I32))
 
-        w_sc_raw = tile("w_sc_raw", [P, S], U8, tag="staged")
+        w_sc_raw = tile("w_sc_raw", [P, S], U8, tag="x_sc_got")
         nc.gpsimd.memset(w_sc_raw[:].bitcast(I32), 0)
         for q in range(4):
             nc.sync.dma_start(
@@ -102,13 +94,18 @@ def tile_picked_hpqhpgateedf_none_po_kernel(
         d_got = tile("d_got", [P, S], U32)
         d_dealt = tile("d_dealt", [P, S], U32)
         nc.vector.tensor_copy(d_got[:], d_win[:].indirect(k1_l[:]))
-        x_got = [tile("x_got%d" % a, [P, HALF_S], U32) for a in range(2)]
-        nc.vector.tensor_copy(x_got[0][:], x_win[:].indirect(offs_l[:, :16]))
+        d_sc = tile("d_sc", [P, S], U8)
+        nc.vector.tensor_copy(
+            d_sc[:].rearrange("p (t c i) -> p c t i", t=4, i=16),
+            d_sc_placed[:].rearrange("p (c i t) -> p c t i", t=4, i=16),
+        )
         nc.vector.tensor_copy(
             d_dealt[:].bitcast(I32).rearrange("p (t c i) -> p c t i", t=4, i=4),
             d_got[:].bitcast(I32).rearrange("p (c i t) -> p c t i", t=4, i=4),
         )
-        nc.vector.tensor_copy(x_got[1][:], x_win[:].indirect(offs_l[:, 16:]))
+        x_got = [tile("x_got%d" % a, [P, HALF_S], U32) for a in range(2)]
+        for a in range(2):
+            nc.vector.tensor_copy(x_got[a][:], x_win[:].indirect(offs_l[:, 16 * a : 16 * (a + 1)]))
 
         w_dealt = tile("w_dealt", [P, 2 * S], U8)
         nc.scalar.copy(
@@ -123,9 +120,9 @@ def tile_picked_hpqhpgateedf_none_po_kernel(
             nc.tensor.matmul_mx(
                 acc[:],
                 lhsT=d_dealt[:, P * t : P * (t + 1)].bitcast(FP8X4),
-                lhsT_scale=scales[:, S + P * t : S + P * (t + 1)],
+                lhsT_scale=d_sc[:, P * t : P * (t + 1)],
                 rhs=x_got[a][:].bitcast(FP8X4),
-                rhs_scale=scales[:, cols],
+                rhs_scale=x_sc[:, cols],
                 start=True,
                 stop=True,
             )
@@ -134,15 +131,16 @@ def tile_picked_hpqhpgateedf_none_po_kernel(
             else:
                 nc.vector.tensor_scalar(h_win[t][:, cols], acc[:], 0.03125, None, ALU.mult)
 
-        lined = tile("lined", [P, 4, HALF_S], F32)
-        small_first = tile("small_first", [P, 4, HALF_V], F32)
+        lined = tile("lined", [P, 5, HALF_S], F32)
+        small_front = tile("small_front", [P, 2, HALF_V], F32)
+        small_back = lined[:, 4, :].rearrange("p (t v) -> p t v", t=2)
         large = tile("large", [P, 4, HALF_V], F32)
         tanh = [tile("tanh%d" % a, [P, 4, HALF_V], F32) for a in range(2)]
-        gate = tile("gate", [P, 4, HALF_V], F32)
+        gate = tile("gate", [P, 4, HALF_V], F32, tag="x_sc_got")
 
         def small(a, ts):
             if a == 0:
-                return small_first[:, ts, :]
+                return small_front[:] if ts.start == 0 else small_back
             if ts.start < 3:
                 return tanh[0][:, ts.start + 1 : ts.stop + 1, :]
             return gate[:, ts, :]
@@ -151,13 +149,17 @@ def tile_picked_hpqhpgateedf_none_po_kernel(
         z_scales = [tile("z_scales%d" % a, [P, HALF_V], U8) for a in range(2)]
 
         def line_up(a, t):
-            nc.scalar.activation(lined[:, t, :], h_win[t][:].indirect(n1_l[:, 16 * a : 16 * (a + 1)]), ACT.Copy)
+            nc.scalar.activation(lined[:, a + t, :], h_win[t][:].indirect(n1_l[:, 16 * a : 16 * (a + 1)]), ACT.Copy)
+
+        def pick(dst, a, ts, op):
+            slots = slice(a + ts.start, a + ts.stop)
+            nc.vector.tensor_tensor(dst, lined[:, slots, 0::2], lined[:, slots, 1::2], op)
 
         def pick_small(a, ts):
-            nc.vector.tensor_tensor(small(a, ts), lined[:, ts, 0::2], lined[:, ts, 1::2], ALU.min)
+            pick(small(a, ts), a, ts, ALU.min)
 
-        def pick_large(ts):
-            nc.vector.tensor_tensor(large[:, ts, :], lined[:, ts, 0::2], lined[:, ts, 1::2], ALU.max)
+        def pick_large(a, ts):
+            pick(large[:, ts, :], a, ts, ALU.max)
 
         def squash(a, ts):
             nc.scalar.activation(tanh[a][:, ts, :], small(a, ts), ACT.Tanh)
@@ -193,14 +195,14 @@ def tile_picked_hpqhpgateedf_none_po_kernel(
         for t in range(4):
             line_up(0, t)
         pick_small(0, front)
-        pick_large(front)
+        pick_large(0, front)
         w_sc = tile("w_sc", [P, S], U8, tag="d_dealt")
         nc.vector.tensor_copy(
             w_sc[:].rearrange("p (t c i) -> p c t i", t=4, i=16),
             w_sc_raw[:].rearrange("p (c i t) -> p c t i", t=4, i=16),
         )
         pick_small(0, back)
-        pick_large(back)
+        pick_large(0, back)
         squash(0, front)
         line_up(1, 0)
         squash(0, back)
@@ -216,7 +218,7 @@ def tile_picked_hpqhpgateedf_none_po_kernel(
         for t in range(4):
             second(h2_a[:, t, :], 0, t)
         pick_small(1, slice(3, 4))
-        pick_large(every)
+        pick_large(1, every)
         squash(1, slice(0, 3))
         squash(1, slice(3, 4))
         for t in range(4):
@@ -242,12 +244,12 @@ def tile_picked_hpqhpgateedf_none_po_kernel(
 
         def keep_first(t):
             nc.vector.tensor_scalar(
-                h2_win[t][:, first], h2_a[:, t, :], 1.0, None, ALU.mult, ALU.max, accum_out=top_a[:, t : t + 1]
+                h_win[t][:, first], h2_a[:, t, :], 1.0, None, ALU.mult, ALU.max, accum_out=top_a[:, t : t + 1]
             )
 
         def keep_last(t):
             nc.vector.tensor_scalar(
-                h2_win[t][:, last], h2_b[t // 2][:, t % 2, :], 1.0, top_a[:, t : t + 1], ALU.mult, ALU.max,
+                h_win[t][:, last], h2_b[t // 2][:, t % 2, :], 1.0, top_a[:, t : t + 1], ALU.mult, ALU.max,
                 accum_out=top[:, t : t + 1],
             )
 
@@ -265,13 +267,13 @@ def tile_picked_hpqhpgateedf_none_po_kernel(
 
         def fetch_top(t):
             nc.scalar.activation(
-                ea[:, t, :], h2_win[t][:].indirect(n2_l[:]), ACT.Exp,
+                ea[:, t, :], h_win[t][:].indirect(n2_l[:]), ACT.Exp,
                 bias=bias_top[:, t : t + 1], scale=tau_sb[:, t : t + 1],
             )
 
         def fetch_low(t, cols):
             nc.scalar.activation(
-                eb[:, t, cols], h2_win[t][:].indirect(n3_l[:, cols.start // 16 : cols.stop // 16]), ACT.Exp,
+                eb[:, t, cols], h_win[t][:].indirect(n3_l[:, cols.start // 16 : cols.stop // 16]), ACT.Exp,
                 bias=bias_low[:, t : t + 1], scale=neg_tau2[:, t : t + 1],
             )
 

@@ -45,32 +45,30 @@ def tile_picked_hpqhpgateedf_none_po_kernel(
         n1_l = lists.tile([P, S // 16], U16, name="n1_l")
         n2_l = lists.tile([P, V // 16], U16, name="n2_l")
         n3_l = lists.tile([P, V // 16], U16, name="n3_l")
-        d_sc_win = tile("d_sc_win", [P, T], U8)
-        x_sc_win = tile("x_sc_win", [P, T], U8)
-        nc.gpsimd.memset(d_sc_win[:].bitcast(I32), 0)
-        nc.scalar.dma_start(d_sc_win[0:P:8, :].bitcast(I32), d_scales[0].bitcast(I32))
-        nc.vector.memset(x_sc_win[:].bitcast(I32), 0)
-        nc.scalar.dma_start(x_sc_win[0:P:8, :].bitcast(I32), x_scales[0].bitcast(I32))
         tau_sb = tile("tau_sb", [P, 4], F32)
         tau2_sb = tile("tau2_sb", [P, 4], F32)
         gn_sb = tile("gn_sb", [P, 4], F32)
         for lst, src in ((k1_l, k1), (offs_l, offs), (n1_l, n1), (n2_l, n2), (n3_l, n3)):
             nc.sync.dma_start(lst[:], src)
         nc.sync.dma_start(tau_sb[:], tau.rearrange("(p t) o -> p (t o)", t=4))
+        d_sc_win = tile("d_sc_win", [P, T], U8)
+        x_sc_win = tile("x_sc_win", [P, T], U8)
+        nc.gpsimd.memset(d_sc_win[:].bitcast(I32), 0)
+        nc.sync.dma_start(d_sc_win[0:P:8, :].bitcast(I32), d_scales[0].bitcast(I32))
+        nc.vector.memset(x_sc_win[:].bitcast(I32), 0)
+        nc.sync.dma_start(x_sc_win[0:P:8, :].bitcast(I32), x_scales[0].bitcast(I32))
 
         d_win = tile("d_win", [P, T], U32)
         x_win = tile("x_win", [P, T], U32)
         w_raw = tile("w_raw", [P, 2 * S], U8)
-        nc.gpsimd.dma_start(d_win[:].bitcast(I32), d_words[0].rearrange("p n r -> p (n r)").bitcast(I32))
-        nc.gpsimd.dma_start(x_win[:].bitcast(I32), x_words[0].rearrange("p n r -> p (n r)").bitcast(I32))
-        nc.gpsimd.dma_start(w_raw[:].bitcast(I32), w1_words[0].bitcast(I32))
-        nc.gpsimd.dma_start(gn_sb[:], gn.rearrange("(p t) o -> p (t o)", t=4))
-        nc.gpsimd.dma_start(tau2_sb[:], tau2.rearrange("(p t) o -> p (t o)", t=4))
+        nc.sync.dma_start(d_win[:].bitcast(I32), d_words[0].rearrange("p n r -> p (n r)").bitcast(I32))
+        nc.sync.dma_start(x_win[:].bitcast(I32), x_words[0].rearrange("p n r -> p (n r)").bitcast(I32))
+        nc.sync.dma_start(w_raw[:].bitcast(I32), w1_words[0].bitcast(I32))
+        for dst, src in ((gn_sb, gn), (tau2_sb, tau2)):
+            nc.sync.dma_start(dst[:], src.rearrange("(p t) o -> p (t o)", t=4))
 
-        d_sc_placed = tile("d_sc_placed", [P, S], U8)
-        x_sc = tile("x_sc", [P, S], U8)
-        nc.vector.memset(d_sc_placed[:].bitcast(I32), 0)
-        nc.vector.memset(x_sc[:].bitcast(I32), 0)
+        scales = tile("scales", [P, 2 * S], U8)
+        nc.vector.memset(scales[:].bitcast(I32), 0)
 
         neg_tau = tile("neg_tau", [P, 4], F32)
         neg_tau2 = tile("neg_tau2", [P, 4], F32)
@@ -79,12 +77,18 @@ def tile_picked_hpqhpgateedf_none_po_kernel(
 
         d_sc_got = tile("d_sc_got", [P, S], U8)
         x_sc_got = tile("x_sc_got", [P, S], U8)
-        for got, win, lst, placed in ((d_sc_got, d_sc_win, k1_l, d_sc_placed), (x_sc_got, x_sc_win, offs_l, x_sc)):
-            nc.vector.tensor_copy(got[:], win[:].indirect(lst[:]))
-            for r in range(4):
-                nc.sync.dma_start(placed[r:P:32, :].bitcast(I32), got[8 * r : P : 32, :].bitcast(I32))
+        staged = tile("staged", [P, 2 * S], U8)
+        nc.vector.tensor_copy(d_sc_got[:], d_sc_win[:].indirect(k1_l[:]))
+        nc.vector.tensor_copy(x_sc_got[:], x_sc_win[:].indirect(offs_l[:]))
+        nc.vector.tensor_copy(
+            staged[:, S:].rearrange("p (t c i) -> p c t i", t=4, i=16),
+            d_sc_got[:].rearrange("p (c i t) -> p c t i", t=4, i=16),
+        )
+        nc.vector.tensor_copy(staged[:, :S].bitcast(I32), x_sc_got[:].bitcast(I32))
+        for r in range(4):
+            nc.scalar.dma_start(scales[r:P:32, :].bitcast(I32), staged[8 * r : P : 32, :].bitcast(I32))
 
-        w_sc_raw = tile("w_sc_raw", [P, S], U8, tag="x_sc_got")
+        w_sc_raw = tile("w_sc_raw", [P, S], U8, tag="staged")
         nc.gpsimd.memset(w_sc_raw[:].bitcast(I32), 0)
         for q in range(4):
             nc.sync.dma_start(
@@ -94,11 +98,6 @@ def tile_picked_hpqhpgateedf_none_po_kernel(
         d_got = tile("d_got", [P, S], U32)
         d_dealt = tile("d_dealt", [P, S], U32)
         nc.vector.tensor_copy(d_got[:], d_win[:].indirect(k1_l[:]))
-        d_sc = tile("d_sc", [P, S], U8)
-        nc.vector.tensor_copy(
-            d_sc[:].rearrange("p (t c i) -> p c t i", t=4, i=16),
-            d_sc_placed[:].rearrange("p (c i t) -> p c t i", t=4, i=16),
-        )
         nc.vector.tensor_copy(
             d_dealt[:].bitcast(I32).rearrange("p (t c i) -> p c t i", t=4, i=4),
             d_got[:].bitcast(I32).rearrange("p (c i t) -> p c t i", t=4, i=4),
@@ -114,15 +113,15 @@ def tile_picked_hpqhpgateedf_none_po_kernel(
         )
 
         h_win = [tile("h_win%d" % t, [P, S], F32) for t in range(4)]
-        for a, t in ((0, 0), (0, 1), (1, 0), (1, 1), (0, 2), (1, 2), (0, 3), (1, 3)):
+        for a, t in ((a, t) for t in range(4) for a in range(2)):
             cols = slice(a * HALF_S, (a + 1) * HALF_S)
             acc = bank(4 * a + t, "h_acc", [P, HALF_S])
             nc.tensor.matmul_mx(
                 acc[:],
                 lhsT=d_dealt[:, P * t : P * (t + 1)].bitcast(FP8X4),
-                lhsT_scale=d_sc[:, P * t : P * (t + 1)],
+                lhsT_scale=scales[:, S + P * t : S + P * (t + 1)],
                 rhs=x_got[a][:].bitcast(FP8X4),
-                rhs_scale=x_sc[:, cols],
+                rhs_scale=scales[:, cols],
                 start=True,
                 stop=True,
             )
@@ -136,7 +135,7 @@ def tile_picked_hpqhpgateedf_none_po_kernel(
         small_back = lined[:, 4, :].rearrange("p (t v) -> p t v", t=2)
         large = tile("large", [P, 4, HALF_V], F32)
         tanh = [tile("tanh%d" % a, [P, 4, HALF_V], F32) for a in range(2)]
-        gate = tile("gate", [P, 4, HALF_V], F32, tag="x_sc_got")
+        gate = tile("gate", [P, 4, HALF_V], F32, tag="staged")
 
         def small(a, ts):
             if a == 0:
@@ -221,8 +220,12 @@ def tile_picked_hpqhpgateedf_none_po_kernel(
         pick_large(1, every)
         squash(1, slice(0, 3))
         squash(1, slice(3, 4))
-        for t in range(4):
-            gain(1, t)
+        for t in range(2):
+            nc.scalar.activation(
+                gate[:, t, :], tanh[1][:, t, :], ACT.Identity, bias=gn_sb[:, t : t + 1], scale=gn_sb[:, t : t + 1]
+            )
+        gain(1, 2)
+        gain(1, 3)
 
         top_a = tile("top_a", [P, 4], F32)
         top = tile("top", [P, 4], F32)
@@ -249,15 +252,15 @@ def tile_picked_hpqhpgateedf_none_po_kernel(
 
         def keep_last(t):
             nc.vector.tensor_scalar(
-                h_win[t][:, last], h2_b[t // 2][:, t % 2, :], 1.0, top_a[:, t : t + 1], ALU.mult, ALU.max,
+                h_win[t][:, last], h2_b[t], 1.0, top_a[:, t : t + 1], ALU.mult, ALU.max,
                 accum_out=top[:, t : t + 1],
             )
 
         def top_bias(ts):
             nc.vector.tensor_tensor(bias_top[:, ts], top[:, ts], neg_tau[:, ts], ALU.mult)
 
-        def lowest_last(ts):
-            nc.vector.tensor_reduce(low_b[:, ts], h2_b[ts.start // 2][:], AXIS_X, ALU.min)
+        def lowest_last(ts, h2):
+            nc.vector.tensor_reduce(low_b[:, ts], h2, AXIS_X, ALU.min)
 
         def lowest(ts):
             nc.vector.tensor_tensor(low[:, ts], low_a[:, ts], low_b[:, ts], ALU.min)
@@ -300,9 +303,12 @@ def tile_picked_hpqhpgateedf_none_po_kernel(
         make_z(1)
         keep_first(1)
         quantise_z(1)
-        h2_b = [bank(1 + u, "h2_b", [P, 2, HALF_V]) for u in range(2)]
+        h2_b0 = bank(1, "h2_b0", [P, HALF_V])
+        h2_b1 = bank(2, "h2_b1", [P, HALF_V])
+        h2_b23 = bank(3, "h2_b23", [P, 2, HALF_V])
+        h2_b = [h2_b0[:], h2_b1[:], h2_b23[:, 0, :], h2_b23[:, 1, :]]
         for t in range(4):
-            second(h2_b[t // 2][:, t % 2, :], 1, t)
+            second(h2_b[t], 1, t)
         nc.vector.tensor_reduce(low_a[:], h2_a[:], AXIS_X, ALU.min)
         keep_last(0)
         keep_last(1)
@@ -310,7 +316,8 @@ def tile_picked_hpqhpgateedf_none_po_kernel(
         top_bias(slice(1, 2))
         fetch_top(0)
         fetch_top(1)
-        lowest_last(front)
+        lowest_last(slice(0, 1), h2_b[0])
+        lowest_last(slice(1, 2), h2_b[1])
         keep_first(2)
         lowest(front)
         keep_first(3)
@@ -319,30 +326,31 @@ def tile_picked_hpqhpgateedf_none_po_kernel(
         fetch_low(1, whole)
         keep_last(2)
         keep_last(3)
-        lowest_last(back)
+        lowest_last(back, h2_b23[:])
         top_bias(back)
         lowest(back)
         fetch_top(2)
         fetch_top(3)
-        add_both(front, whole)
+        add_both(slice(0, 1), whole)
         low_bias(back)
         for cols in (first, last):
             fetch_low(2, cols)
             fetch_low(3, cols)
-        finish(front, first, h2_a[:, front, :])
-        finish(front, last, h2_b[0][:])
+        add_both(slice(1, 2), whole)
+        for t in range(2):
+            finish(slice(t, t + 1), whole, h_win[t][:, whole])
         nc.sync.dma_start(out_rows[:, front, :], res[:, front, :])
         round_res(nc.vector.tensor_copy, front, whole)
         add_both(back, first)
         add_both(slice(2, 3), last)
+        add_both(slice(3, 4), last)
         finish(back, first, h2_a[:, back, :])
         nc.sync.dma_start(out_rows[:, back, first], res[:, back, first])
-        add_both(slice(3, 4), last)
-        round_res(nc.scalar.copy, back, first)
-        finish(back, last, h2_b[1][:])
+        finish(back, last, h2_b23[:])
         nc.sync.dma_start(out_rows[:, back, last], res[:, back, last])
+        round_res(nc.scalar.copy, back, first)
+        round_res(nc.vector.tensor_copy, back, last)
         planes(first)
-        round_res(nc.scalar.copy, back, last)
         planes(last)
         for q in range(4):
             eng = nc.scalar if q % 2 == 0 else nc.sync

from contextlib import ExitStack

import concourse.mybir as mybir

FLOPS = 402653184

F32 = mybir.dt.float32
BF16 = mybir.dt.bfloat16
I32 = mybir.dt.int32
U32 = mybir.dt.uint32
U16 = mybir.dt.uint16
U8 = mybir.dt.uint8
FP8X4 = mybir.dt.float8_e4m3fn_x4
FP4X4 = mybir.dt.float4_e2m1fn_x4
ALU = mybir.AluOpType
ACT = mybir.ActivationFunctionType
AXIS_X = mybir.AxisListType.X

P = 128
T = 2048
S = 512
V = 256
HALF_S = S // 2
HALF_V = V // 2


def tile_picked_hpqhpgateedf_none_po_kernel(
    tc, x_words, x_scales, d_words, d_scales, gn, w1_words, w1_scales, tau, tau2,
    offs, k1, n1, n2, n3, out_0, out_1, out_2,
):
    nc = tc.nc
    with ExitStack() as ctx:
        lists = ctx.enter_context(tc.tile_pool(name="lists", bufs=1))
        sb = ctx.enter_context(tc.tile_pool(name="sb", bufs=1))
        ps = ctx.enter_context(tc.psum_pool(name="ps", bufs=1))

        def tile(name, shape, dtype, tag=None):
            return sb.tile(shape, dtype, name=name, tag=tag or name, align_bytes=64)

        def bank(b, name, shape):
            return ps.tile(shape, F32, name=name, tag="bank%d" % b)

        k1_l = lists.tile([P, S // 16], U16, name="k1_l")
        offs_l = lists.tile([P, S // 16], U16, name="offs_l")
        n1_l = lists.tile([P, S // 16], U16, name="n1_l")
        n2_l = lists.tile([P, V // 16], U16, name="n2_l")
        n3_l = lists.tile([P, V // 16], U16, name="n3_l")
        tau_sb = tile("tau_sb", [P, 4], F32)
        tau2_sb = tile("tau2_sb", [P, 4], F32)
        gn_sb = tile("gn_sb", [P, 4], F32)
        for lst, src in ((k1_l, k1), (offs_l, offs), (n1_l, n1), (n2_l, n2), (n3_l, n3)):
            nc.sync.dma_start(lst[:], src)
        nc.sync.dma_start(tau_sb[:], tau.rearrange("(p t) o -> p (t o)", t=4))
        d_sc_win = tile("d_sc_win", [P, T], U8)
        x_sc_win = tile("x_sc_win", [P, T], U8)
        nc.gpsimd.memset(d_sc_win[:].bitcast(I32), 0)
        nc.sync.dma_start(d_sc_win[0:P:8, :].bitcast(I32), d_scales[0].bitcast(I32))
        nc.vector.memset(x_sc_win[:].bitcast(I32), 0)
        nc.sync.dma_start(x_sc_win[0:P:8, :].bitcast(I32), x_scales[0].bitcast(I32))

        d_win = tile("d_win", [P, T], U32)
        x_win = tile("x_win", [P, T], U32)
        w_raw = tile("w_raw", [P, 2 * S], U8)
        nc.sync.dma_start(d_win[:].bitcast(I32), d_words[0].rearrange("p n r -> p (n r)").bitcast(I32))
        nc.sync.dma_start(x_win[:].bitcast(I32), x_words[0].rearrange("p n r -> p (n r)").bitcast(I32))
        nc.sync.dma_start(w_raw[:].bitcast(I32), w1_words[0].bitcast(I32))
        for dst, src in ((gn_sb, gn), (tau2_sb, tau2)):
            nc.sync.dma_start(dst[:], src.rearrange("(p t) o -> p (t o)", t=4))

        scales = tile("scales", [P, 2 * S], U8)
        nc.vector.memset(scales[:].bitcast(I32), 0)

        neg_tau = tile("neg_tau", [P, 4], F32)
        neg_tau2 = tile("neg_tau2", [P, 4], F32)
        nc.scalar.activation(neg_tau[:], tau_sb[:], ACT.Copy, scale=-1.0)
        nc.gpsimd.tensor_scalar(neg_tau2[:], tau2_sb[:], -1.0, 0.0, ALU.mult, ALU.add)

        d_sc_got = tile("d_sc_got", [P, S], U8)
        x_sc_got = tile("x_sc_got", [P, S], U8)
        staged = tile("staged", [P, 2 * S], U8)
        nc.vector.tensor_copy(d_sc_got[:], d_sc_win[:].indirect(k1_l[:]))
        nc.vector.tensor_copy(x_sc_got[:], x_sc_win[:].indirect(offs_l[:]))
        nc.vector.tensor_copy(
            staged[:, S:].rearrange("p (t c i) -> p c t i", t=4, i=16),
            d_sc_got[:].rearrange("p (c i t) -> p c t i", t=4, i=16),
        )
        nc.vector.tensor_copy(staged[:, :S].bitcast(I32), x_sc_got[:].bitcast(I32))
        for r in range(4):
            nc.scalar.dma_start(scales[r:P:32, :].bitcast(I32), staged[8 * r : P : 32, :].bitcast(I32))

        w_sc_raw = tile("w_sc_raw", [P, S], U8, tag="staged")
        nc.gpsimd.memset(w_sc_raw[:].bitcast(I32), 0)
        for q in range(4):
            nc.sync.dma_start(
                w_sc_raw[32 * q : 32 * q + 4, :].bitcast(I32), w1_scales[0, 4 * q : 4 * q + 4, :].bitcast(I32)
            )

        d_got = tile("d_got", [P, S], U32)
        d_dealt = tile("d_dealt", [P, S], U32)
        nc.vector.tensor_copy(d_got[:], d_win[:].indirect(k1_l[:]))
        nc.vector.tensor_copy(
            d_dealt[:].bitcast(I32).rearrange("p (t c i) -> p c t i", t=4, i=4),
            d_got[:].bitcast(I32).rearrange("p (c i t) -> p c t i", t=4, i=4),
        )
        x_got = [tile("x_got%d" % a, [P, HALF_S], U32) for a in range(2)]
        for a in range(2):
            nc.vector.tensor_copy(x_got[a][:], x_win[:].indirect(offs_l[:, 16 * a : 16 * (a + 1)]))

        w_dealt = tile("w_dealt", [P, 2 * S], U8)
        nc.scalar.copy(
            w_dealt[:].bitcast(U16).rearrange("p (t c i) -> p c t i", t=4, i=8),
            w_raw[:].bitcast(U16).rearrange("p (c i t) -> p c t i", t=4, i=8),
        )

        h_win = [tile("h_win%d" % t, [P, S], F32) for t in range(4)]
        for a, t in ((a, t) for t in range(4) for a in range(2)):
            cols = slice(a * HALF_S, (a + 1) * HALF_S)
            acc = bank(4 * a + t, "h_acc", [P, HALF_S])
            nc.tensor.matmul_mx(
                acc[:],
                lhsT=d_dealt[:, P * t : P * (t + 1)].bitcast(FP8X4),
                lhsT_scale=scales[:, S + P * t : S + P * (t + 1)],
                rhs=x_got[a][:].bitcast(FP8X4),
                rhs_scale=scales[:, cols],
                start=True,
                stop=True,
            )
            if a == 0 and t < 2:
                nc.scalar.activation(h_win[t][:, cols], acc[:], ACT.Copy, scale=0.03125)
            else:
                nc.vector.tensor_scalar(h_win[t][:, cols], acc[:], 0.03125, None, ALU.mult)

        lined = tile("lined", [P, 5, HALF_S], F32)
        small_front = tile("small_front", [P, 2, HALF_V], F32)
        small_back = lined[:, 4, :].rearrange("p (t v) -> p t v", t=2)
        large = tile("large", [P, 4, HALF_V], F32)
        tanh = [tile("tanh%d" % a, [P, 4, HALF_V], F32) for a in range(2)]
        gate = tile("gate", [P, 4, HALF_V], F32, tag="staged")

        def small(a, ts):
            if a == 0:
                return small_front[:] if ts.start == 0 else small_back
            if ts.start < 3:
                return tanh[0][:, ts.start + 1 : ts.stop + 1, :]
            return gate[:, ts, :]
        z_bf = [tile("z_bf%d" % a, [P, HALF_V, 4], BF16) for a in range(2)]
        z_codes = [tile("z_codes%d" % a, [P, HALF_V], U32) for a in range(2)]
        z_scales = [tile("z_scales%d" % a, [P, HALF_V], U8) for a in range(2)]

        def line_up(a, t):
            nc.scalar.activation(lined[:, a + t, :], h_win[t][:].indirect(n1_l[:, 16 * a : 16 * (a + 1)]), ACT.Copy)

        def pick(dst, a, ts, op):
            slots = slice(a + ts.start, a + ts.stop)
            nc.vector.tensor_tensor(dst, lined[:, slots, 0::2], lined[:, slots, 1::2], op)

        def pick_small(a, ts):
            pick(small(a, ts), a, ts, ALU.min)

        def pick_large(a, ts):
            pick(large[:, ts, :], a, ts, ALU.max)

        def squash(a, ts):
            nc.scalar.activation(tanh[a][:, ts, :], small(a, ts), ACT.Tanh)

        def gain(a, t):
            nc.vector.tensor_scalar(gate[:, t, :], tanh[a][:, t, :], 1.0, gn_sb[:, t : t + 1], ALU.add, ALU.mult)

        def make_z(a):
            nc.vector.tensor_tensor(
                z_bf[a][:].rearrange("p (c i) t -> p c t i", i=4),
                gate[:].rearrange("p t (c i) -> p c t i", i=4),
                large[:].rearrange("p t (c i) -> p c t i", i=4),
                ALU.mult,
            )

        def quantise_z(a):
            nc.vector.quantize_mx(
                z_codes[a][:].bitcast(FP8X4), z_scales[a][:], z_bf[a][:].rearrange("p v t -> p (v t)")
            )

        def second(acc, a, t):
            nc.tensor.matmul_mx(
                acc,
                lhsT=w_dealt[:, 2 * P * t : 2 * P * (t + 1)].bitcast(FP4X4),
                lhsT_scale=w_sc[:, P * t : P * (t + 1)],
                rhs=z_codes[a][:].bitcast(FP8X4),
                rhs_scale=z_scales[a][:],
                start=True,
                stop=True,
            )

        every, front, back = slice(0, 4), slice(0, 2), slice(2, 4)
        for t in range(4):
            line_up(0, t)
        pick_small(0, front)
        pick_large(0, front)
        w_sc = tile("w_sc", [P, S], U8, tag="d_dealt")
        nc.vector.tensor_copy(
            w_sc[:].rearrange("p (t c i) -> p c t i", t=4, i=16),
            w_sc_raw[:].rearrange("p (c i t) -> p c t i", t=4, i=16),
        )
        pick_small(0, back)
        pick_large(0, back)
        squash(0, front)
        line_up(1, 0)
        squash(0, back)
        for t in range(1, 4):
            line_up(1, t)
        for t in range(4):
            gain(0, t)
        pick_small(1, slice(0, 1))
        make_z(0)
        pick_small(1, slice(1, 3))
        quantise_z(0)
        h2_a = bank(0, "h2_a", [P, 4, HALF_V])
        for t in range(4):
            second(h2_a[:, t, :], 0, t)
        pick_small(1, slice(3, 4))
        pick_large(1, every)
        squash(1, slice(0, 3))
        squash(1, slice(3, 4))
        for t in range(2):
            nc.scalar.activation(
                gate[:, t, :], tanh[1][:, t, :], ACT.Identity, bias=gn_sb[:, t : t + 1], scale=gn_sb[:, t : t + 1]
            )
        gain(1, 2)
        gain(1, 3)

        top_a = tile("top_a", [P, 4], F32)
        top = tile("top", [P, 4], F32)
        low_a = tile("low_a", [P, 4], F32)
        low_b = tile("low_b", [P, 4], F32)
        low = tile("low", [P, 4], F32)
        bias_top = tile("bias_top", [P, 4], F32)
        bias_low = tile("bias_low", [P, 4], F32)
        ea = tile("ea", [P, 4, V], F32)
        eb = tile("eb", [P, 4, V], F32)
        both = tile("both", [P, 4, V], F32)
        res = tile("res", [P, 4, V], F32)
        res_bf = tile("res_bf", [P, V, 4], BF16)
        out_codes = tile("out_codes", [P, V], U32)
        out_scales = tile("out_scales", [P, V], U8)
        out_rows = out_0.rearrange("(p t) v -> p t v", t=4)
        out_words = out_1[0].rearrange("p v r -> p (v r)").bitcast(I32)
        first, last, whole = slice(0, HALF_V), slice(HALF_V, V), slice(0, V)

        def keep_first(t):
            nc.vector.tensor_scalar(
                h_win[t][:, first], h2_a[:, t, :], 1.0, None, ALU.mult, ALU.max, accum_out=top_a[:, t : t + 1]
            )

        def keep_last(t):
            nc.vector.tensor_scalar(
                h_win[t][:, last], h2_b[t], 1.0, top_a[:, t : t + 1], ALU.mult, ALU.max,
                accum_out=top[:, t : t + 1],
            )

        def top_bias(ts):
            nc.vector.tensor_tensor(bias_top[:, ts], top[:, ts], neg_tau[:, ts], ALU.mult)

        def lowest_last(ts, h2):
            nc.vector.tensor_reduce(low_b[:, ts], h2, AXIS_X, ALU.min)

        def lowest(ts):
            nc.vector.tensor_tensor(low[:, ts], low_a[:, ts], low_b[:, ts], ALU.min)

        def low_bias(ts):
            nc.vector.tensor_tensor(bias_low[:, ts], low[:, ts], tau2_sb[:, ts], ALU.mult)

        def fetch_top(t):
            nc.scalar.activation(
                ea[:, t, :], h_win[t][:].indirect(n2_l[:]), ACT.Exp,
                bias=bias_top[:, t : t + 1], scale=tau_sb[:, t : t + 1],
            )

        def fetch_low(t, cols):
            nc.scalar.activation(
                eb[:, t, cols], h_win[t][:].indirect(n3_l[:, cols.start // 16 : cols.stop // 16]), ACT.Exp,
                bias=bias_low[:, t : t + 1], scale=neg_tau2[:, t : t + 1],
            )

        def add_both(ts, cols):
            nc.vector.tensor_tensor(both[:, ts, cols], ea[:, ts, cols], eb[:, ts, cols], ALU.add)

        def finish(ts, cols, h2):
            nc.vector.scalar_tensor_tensor(res[:, ts, cols], h2, 1.5, both[:, ts, cols], ALU.mult, ALU.mult)

        def round_res(copy, ts, cols):
            copy(
                res_bf[:, cols, ts].rearrange("p (c i) t -> p c t i", i=4),
                res[:, ts, cols].rearrange("p t (c i) -> p c t i", i=4),
            )

        def planes(cols):
            nc.vector.quantize_mx(
                out_codes[:, cols].bitcast(FP8X4), out_scales[:, cols],
                res_bf[:, cols, :].rearrange("p v t -> p (v t)"),
            )
            nc.sync.dma_start(out_words[:, cols], out_codes[:, cols].bitcast(I32))

        keep_first(0)
        make_z(1)
        keep_first(1)
        quantise_z(1)
        h2_b0 = bank(1, "h2_b0", [P, HALF_V])
        h2_b1 = bank(2, "h2_b1", [P, HALF_V])
        h2_b23 = bank(3, "h2_b23", [P, 2, HALF_V])
        h2_b = [h2_b0[:], h2_b1[:], h2_b23[:, 0, :], h2_b23[:, 1, :]]
        for t in range(4):
            second(h2_b[t], 1, t)
        nc.vector.tensor_reduce(low_a[:], h2_a[:], AXIS_X, ALU.min)
        keep_last(0)
        keep_last(1)
        top_bias(slice(0, 1))
        top_bias(slice(1, 2))
        fetch_top(0)
        fetch_top(1)
        lowest_last(slice(0, 1), h2_b[0])
        lowest_last(slice(1, 2), h2_b[1])
        keep_first(2)
        lowest(front)
        keep_first(3)
        low_bias(front)
        fetch_low(0, whole)
        fetch_low(1, whole)
        keep_last(2)
        keep_last(3)
        lowest_last(back, h2_b23[:])
        top_bias(back)
        lowest(back)
        fetch_top(2)
        fetch_top(3)
        add_both(slice(0, 1), whole)
        low_bias(back)
        for cols in (first, last):
            fetch_low(2, cols)
            fetch_low(3, cols)
        add_both(slice(1, 2), whole)
        for t in range(2):
            finish(slice(t, t + 1), whole, h_win[t][:, whole])
        nc.sync.dma_start(out_rows[:, front, :], res[:, front, :])
        round_res(nc.vector.tensor_copy, front, whole)
        add_both(back, first)
        add_both(slice(2, 3), last)
        add_both(slice(3, 4), last)
        finish(back, first, h2_a[:, back, :])
        nc.sync.dma_start(out_rows[:, back, first], res[:, back, first])
        finish(back, last, h2_b23[:])
        nc.sync.dma_start(out_rows[:, back, last], res[:, back, last])
        round_res(nc.scalar.copy, back, first)
        round_res(nc.vector.tensor_copy, back, last)
        planes(first)
        planes(last)
        for q in range(4):
            eng = nc.scalar if q % 2 == 0 else nc.sync
            eng.dma_start(out_2[0, 4 * q : 4 * q + 4, :].bitcast(I32), out_scales[32 * q : 32 * q + 4, :].bitcast(I32))
